import numpy as np
import ml_dtypes


def mxq(x, axis, fmt="e4m3"):
    dtype, down = {"e4m3": (ml_dtypes.float8_e4m3fn, 7), "e5m2": (ml_dtypes.float8_e5m2, 14)}[fmt]
    v = np.moveaxis(np.asarray(x, np.float32).astype(ml_dtypes.bfloat16).astype(np.float64), axis, -1)
    blocks = v.reshape(v.shape[:-1] + (-1, 32))
    amax = np.abs(blocks).max(-1, keepdims=True)
    byte = np.maximum(np.where(amax > 0, np.frexp(amax)[1] - 1 + 127, 0) - down, 1)
    scale = np.exp2(byte - 127.0)
    codes = (blocks / scale).astype(np.float32).astype(dtype).astype(np.float64)
    return np.moveaxis((codes * scale).reshape(v.shape), -1, axis)


WIDE = False


def mx_kscale(k):
    if not WIDE:
        return np.ones(k)
    levels = np.array([10, -10, 5, -5, 0])
    if k % 512:
        return np.exp2(np.random.permutation(np.resize(levels, k // 32))).repeat(32)
    a = np.empty((k // 512, 16))
    for p in range(k // 512):
        a[p, :8] = np.random.permutation(np.resize(levels, 8))
        for g in range(8):
            far = levels[np.abs(levels - a[p, g]) >= 10]
            a[p, g + 8] = far[np.random.randint(len(far))]
    return np.exp2(a.ravel()).repeat(32)


def f64(x):
    return np.asarray(x).astype(np.float64)


def striped(idx):
    return np.tile(idx.reshape(-1, 16).T, (8, 1)).astype(np.uint16)


def unstriped(offs):
    return offs[:16].T.reshape(-1).astype(np.int64)


E2M1 = np.array([0.0, 0.5, 1.0, 1.5, 2.0, 3.0, 4.0, 6.0, -0.0, -0.5, -1.0, -1.5, -2.0, -3.0, -4.0, -6.0])


def pack_weight(w, fmt):
    k, n = w.shape
    w = f64(np.asarray(w, np.float32).astype(ml_dtypes.bfloat16)).reshape(k // 32, 32, n)
    amax = np.abs(w).max(1)
    if fmt == "e4m3":
        byte = np.frexp(amax)[1] - 1 + 127 - 7
    else:
        mant, ex = np.frexp(amax / 6.0)
        byte = np.where(mant > 0.5, ex, ex - 1) + 127
    byte = np.clip(np.where(amax > 0, byte, 1), 1, 254)
    scaled = (w * np.exp2(127.0 - byte)[:, None, :]).reshape(k, n).astype(np.float32)
    by_word = np.ascontiguousarray(scaled.reshape(k // 512, 128, 4, n).transpose(0, 1, 3, 2))
    if fmt == "e4m3":
        words = by_word.astype(ml_dtypes.float8_e4m3fn).view(np.uint8)
    else:
        c = by_word.astype(ml_dtypes.float4_e2m1fn).view(np.uint8) & 0xF
        words = (c[..., 0::2] | (c[..., 1::2] << 4)).reshape(k // 512, 128, 2 * n)
    return np.ascontiguousarray(words), np.ascontiguousarray(byte.astype(np.uint8).reshape(k // 512, 16, n))


def unpack_weight(words, scales, fmt):
    g, _, n = scales.shape
    words = np.ascontiguousarray(words).reshape(g, 128, n, -1)
    if fmt == "e4m3":
        vals = words.view(ml_dtypes.float8_e4m3fn).astype(np.float64)
    else:
        nib = np.empty((g, 128, n, 4), np.uint8)
        nib[..., 0::2] = words & 0xF
        nib[..., 1::2] = words >> 4
        vals = E2M1[nib]
    vals = vals * np.repeat(np.exp2(scales.astype(np.float64) - 127.0), 8, axis=1)[..., None]
    return vals.transpose(0, 1, 3, 2).reshape(g * 512, n)


def gelu(v):
    return 0.5 * v * (1.0 + np.tanh(np.sqrt(2.0 / np.pi) * (v + 0.044715 * v**3)))


def pack_table4(v):
    words, scales = pack_weight(v, "e2m1")
    g, t = words.shape[0] // 2, v.shape[1]
    words = words.reshape(g, 2, 128, t, 2).transpose(0, 2, 3, 1, 4)
    return np.concatenate([words.reshape(g, -1), scales.reshape(g, -1)], axis=1)


def unpack_table4(tab):
    g, t = tab.shape[0], tab.shape[1] // 544
    words = tab[:, :512 * t].reshape(g, 128, t, 2, 2).transpose(0, 3, 1, 2, 4).reshape(2 * g, 128, 2 * t)
    return unpack_weight(words, tab[:, 512 * t:].reshape(2 * g, 16, t), "e2m1")


K, H, N, T, S = 1024, 1536, 384, 4096, 1024

def setup_inputs():
    n = np.random.standard_normal
    s = mx_kscale(K)[:, None]
    u = mx_kscale(H)[:, None]
    tab = pack_table4(n((K, T)) * s)
    w1_words, w1_scales = pack_weight(n((K, H)) / np.sqrt(K) / s, "e2m1")
    gain = (np.exp(0.3 * n(H)) * u[:, 0]).astype(np.float32)
    w2 = (n((H, N)) / np.sqrt(H) / u).astype(np.float32)
    bias = (0.5 * n(N)).astype(np.float32)
    offs = striped(np.random.permutation(T)[:S])
    return {"tab": tab, "w1_words": w1_words, "w1_scales": w1_scales,
            "gain": gain, "w2": w2, "bias": bias, "offs": offs}

def reference(tab, w1_words, w1_scales, gain, w2, bias, offs):
    v = unpack_table4(tab)[:, unstriped(offs)]
    w1 = unpack_weight(w1_words, w1_scales, "e2m1")
    a = w1.T @ v
    depth = np.abs(a)
    h = f64(gain)[:, None] * np.exp(-depth)
    hq = mxq(h, 0, "e4m3")
    w2q = mxq(f64(w2), 0, "e4m3")
    y = w2q.T @ hq
    return y + f64(bias)[:, None]

@@ -1,0 +1,263 @@
+from contextlib import ExitStack
+
+import concourse.mybir as mybir
+from concourse.masks import make_identity
+
+K, H, N, T, S = 1024, 1536, 384, 4096, 1024
+FLOPS = 2 * K * H * S + 2 * H * N * S
+
+F32 = mybir.dt.float32
+BF16 = mybir.dt.bfloat16
+I32 = mybir.dt.int32
+U32 = mybir.dt.uint32
+U16 = mybir.dt.uint16
+U8 = mybir.dt.uint8
+FP8X4 = mybir.dt.float8_e4m3fn_x4
+FP4X4 = mybir.dt.float4_e2m1fn_x4
+ACT = mybir.ActivationFunctionType
+ALU = mybir.AluOpType
+
+P = 128
+HB = H // 512
+NC = N // P
+HALF = 512
+CH = 256
+NQ = S // CH
+
+
+def tile_list_voxel_transmittance_decode_kernel(tc, tab, w1_words, w1_scales, gain, w2, bias, offs, out):
+    nc = tc.nc
+    with ExitStack() as ctx:
+        keep = ctx.enter_context(tc.tile_pool(name="keep", bufs=1))
+        ring = ctx.enter_context(tc.tile_pool(name="ring", bufs=3))
+        psum_a = ctx.enter_context(tc.psum_pool(name="psum_a", bufs=5))
+        psum_y = ctx.enter_context(tc.psum_pool(name="psum_y", bufs=3))
+
+        offsets = keep.tile([P, S // 16], U16, name="offsets")
+        nc.sync.dma_start(offsets[:], offs)
+
+        tab_scales = keep.tile([P, T // 4], I32, name="tab_scales", align_bytes=64)
+        nc.vector.memset(tab_scales[:], 0)
+        w1s_raw = keep.tile([P, 2, H // 4], I32, name="w1s_raw", align_bytes=64)
+        nc.vector.memset(w1s_raw[:], 0)
+        rows = keep.tile([P, N], F32, name="rows")
+        nc.vector.memset(rows[:], 0.0)
+        vs1 = [keep.tile([P, HALF // 4], I32, name="vs1_%d" % hf, align_bytes=64) for hf in range(2)]
+        for hf in range(2):
+            nc.vector.memset(vs1[hf][:], 0)
+
+        zeros = keep.tile([P, 8], F32, name="zeros")
+        nc.gpsimd.memset(zeros[:], 0.0)
+        warm = keep.tile([P, 8], F32, name="warm")
+        nc.scalar.activation(out=warm[:], in_=zeros[:], func=ACT.Exp)
+
+        w1_view = w1_words.rearrange("a p n -> p a n")
+        w1w_raw = [keep.tile([P, 2, 256], I32, name="w1w_raw%d" % b, align_bytes=64) for b in range(HB)]
+        nc.sync.dma_start(w1w_raw[0][:], w1_view[:, :, 0:1024].bitcast(I32))
+
+        scale_rows = tab[0, 512 * T:].rearrange("(h q r t) -> r q h t", h=2, q=4, r=4)
+        for r in range(4):
+            nc.sync.dma_start(tab_scales[r:P:16, :], scale_rows[r].bitcast(I32))
+        tab_words = keep.tile([P, T], I32, name="tab_words", align_bytes=64)
+        nc.sync.dma_start(tab_words[:], tab[0, 0:512 * T].rearrange("(p x) -> p x", p=P).bitcast(I32))
+
+        for q in range(4):
+            nc.gpsimd.dma_start(
+                w1s_raw[32 * q:32 * q + 4, :, :],
+                w1_scales[:, 4 * q:4 * q + 4, :].rearrange("a r c -> r a c").bitcast(I32),
+            )
+        ident = keep.tile([P, P], F32, name="ident")
+        make_identity(nc, ident[:])
+
+        nc.sync.dma_start(
+            rows[0:4, :].rearrange("j (m i) -> j m i", i=8),
+            gain.rearrange("(m j i) -> j m i", j=4, i=8),
+        )
+        nc.sync.dma_start(rows[4:5, :], bias.rearrange("(o n) -> o n", o=1))
+        for b in range(1, HB):
+            nc.sync.dma_start(w1w_raw[b][:], w1_view[:, :, 1024 * b:1024 * (b + 1)].bitcast(I32))
+        w2_raw = [keep.tile([P, 4, N], F32, name="w2_raw%d" % b) for b in range(HB)]
+        w2_view = w2.rearrange("(b g j i) n -> b j g i n", b=HB, j=4, i=8)
+        for b in range(HB):
+            for j in range(4):
+                nc.sync.dma_start(w2_raw[b][:, j, :], w2_view[b, j])
+
+        vs0 = [keep.tile([P, HALF], U8, name="vs0_%d" % hf, align_bytes=64) for hf in range(2)]
+        picked = [keep.tile([P, HALF], U32, name="picked%d" % hf, align_bytes=64) for hf in range(2)]
+        vw = [keep.tile([P, 2, 2 * HALF], U8, name="vw%d" % hf, align_bytes=64) for hf in range(2)]
+
+        def gather_scales(hf):
+            part = offsets[:, hf * HALF // 16:(hf + 1) * HALF // 16]
+            nc.vector.tensor_copy(vs0[hf][:], tab_scales[:].bitcast(U8).indirect(part))
+            nc.gpsimd.dma_start(vs1[hf][0:112, :], vs0[hf][16:P, :].bitcast(I32))
+
+        def gather_words(hf):
+            part = offsets[:, hf * HALF // 16:(hf + 1) * HALF // 16]
+            nc.vector.tensor_copy(picked[hf][:], tab_words[:].bitcast(U32).indirect(part))
+
+        def part_words(hf):
+            nc.vector.tensor_copy(
+                vw[hf][:].bitcast(U16),
+                picked[hf][:].bitcast(U16).rearrange("p (s a) -> p a s", a=2),
+            )
+
+        w1w = [keep.tile([P, 2, 256], I32, name="w1w%d" % b, align_bytes=64) for b in range(HB)]
+        w1s = keep.tile([P, 2 * HB, 128], I32, name="w1s", align_bytes=64)
+
+        def order_w1_words(b):
+            for a in range(2):
+                nc.vector.tensor_copy(
+                    w1w[b][:, a, :].rearrange("p (j g i) -> p j g i", j=4, g=16),
+                    w1w_raw[b][:, a, :].rearrange("p (g j i) -> p j g i", j=4, g=16),
+                )
+
+        def order_w1_scales():
+            src = w1s_raw[:].rearrange("p a (b g j i) -> p j (a b) g i", b=HB, g=16, j=4)
+            dst = w1s[:].rearrange("p m (j g i) -> p j m g i", j=4, g=16)
+            for j in range(4):
+                nc.vector.tensor_copy(dst[:, j], src[:, j])
+
+        w2w = keep.tile([P, HB, N], U32, name="w2w", align_bytes=64)
+        w2s = keep.tile([P, HB, N], U8, name="w2s", align_bytes=64)
+        w2_bf = [keep.tile([P, N, 4], BF16, name="w2_bf%d" % b, align_bytes=64) for b in range(HB)]
+
+        def round_w2(b):
+            nc.vector.tensor_copy(w2_bf[b][:], w2_raw[b][:].rearrange("p j n -> p n j"))
+
+        def quantize_w2(b):
+            flat = w2_bf[b][:].rearrange("p n j -> p (n j)")
+            for c0, c1 in ((0, 256), (256, N)):
+                nc.vector.quantize_mx(
+                    out=w2w[:, b, c0:c1].bitcast(FP8X4), scales=w2s[:, b, c0:c1], in_=flat[:, 4 * c0:4 * c1]
+                )
+
+        gather_scales(0)
+        order_w1_words(0)
+        gather_scales(1)
+        order_w1_scales()
+        gather_words(0)
+        part_words(0)
+
+        consts = keep.tile([P, HB, 8], F32, name="consts")
+        turned = psum_y.tile([P, 4, P], F32, name="turned", tag="y")
+        for b in range(HB):
+            nc.tensor.transpose(turned[:, b, :], rows[:, P * b:P * (b + 1)], ident[:])
+        nc.scalar.copy(consts[:], turned[:, 0:HB, 0:8])
+
+        units = [(q, b) for q in range(NQ) for b in range(HB)]
+        banks, depth, trans, hb, hw, hs, acc, res = {}, {}, {}, {}, {}, {}, {}, {}
+
+        def pieces(u):
+            return ((0, CH // 2), (CH // 2, CH)) if u == len(units) - 1 else ((0, CH),)
+
+        def densities(u, half):
+            q, b = units[u]
+            hf, c0 = q // 2, (q % 2) * CH
+            bank = psum_a.tile([P, 2, CH], F32, name="bank", tag="a")
+            banks[u, half] = bank
+            for e in range(2):
+                j = 2 * half + e
+                for a in range(2):
+                    plane = vs0[hf][:] if a == 0 else vs1[hf][:].bitcast(U8)
+                    nc.tensor.matmul_mx(
+                        out=bank[:, e, :],
+                        lhsT=w1w[b][:, a, 64 * j:64 * (j + 1)].bitcast(U8).bitcast(FP4X4),
+                        lhsT_scale=w1s[:, a * HB + b, 32 * j:32 * (j + 1)].bitcast(U8),
+                        rhs=vw[hf][:, a, 2 * c0:2 * (c0 + CH)].bitcast(FP4X4),
+                        rhs_scale=plane[:, c0:c0 + CH],
+                        start=(a == 0),
+                        stop=(a == 1),
+                    )
+
+        def depths(u, half):
+            if half == 0:
+                depth[u] = ring.tile([P, 2, CH, 2], F32, name="depth", tag="depth")
+            nc.scalar.activation(
+                out=depth[u][:, half], in_=banks[u, half][:].rearrange("p e n -> p n e"), func=ACT.Abs
+            )
+
+        def transmittances(u):
+            trans[u] = ring.tile([P, 2, CH, 2], F32, name="trans", tag="trans", bufs=6)
+            for n0, n1 in pieces(u):
+                nc.scalar.activation(
+                    out=trans[u][:, :, n0:n1, :], in_=depth[u][:, :, n0:n1, :], func=ACT.Exp, scale=-1.0
+                )
+
+        def gained(u):
+            b = units[u][1]
+            hb[u] = ring.tile([P, CH, 2, 2], BF16, name="hb", tag="hb", align_bytes=64)
+            for n0, n1 in pieces(u):
+                g = consts[:, b, 0:4].rearrange("p (u e) -> p u e", u=2).unsqueeze(1).to_broadcast([P, n1 - n0, 2, 2])
+                nc.vector.tensor_tensor(
+                    hb[u][:, n0:n1], trans[u][:, :, n0:n1, :].rearrange("p u n e -> p n u e"), g, ALU.mult
+                )
+
+        def quantize_h(u):
+            hw[u] = keep.tile([P, CH], U32, name="hw%d" % u, align_bytes=64)
+            hs[u] = keep.tile([P, CH], U8, name="hs%d" % u, align_bytes=64)
+            for n0, n1 in pieces(u):
+                nc.vector.quantize_mx(
+                    out=hw[u][:, n0:n1].bitcast(FP8X4),
+                    scales=hs[u][:, n0:n1],
+                    in_=hb[u][:, n0:n1].rearrange("p n u e -> p (n u e)"),
+                )
+
+        def decode(u):
+            q, b = units[u]
+            for c in range(NC):
+                if b == 0:
+                    acc[q, c] = psum_y.tile([P, 2 * CH], F32, name="acc", tag="y")
+                nc.tensor.matmul_mx(
+                    out=acc[q, c][:, 0:CH],
+                    lhsT=w2w[:, b, P * c:P * (c + 1)].bitcast(FP8X4),
+                    lhsT_scale=w2s[:, b, P * c:P * (c + 1)],
+                    rhs=hw[u][:].bitcast(FP8X4),
+                    rhs_scale=hs[u][:],
+                    start=(b == 0),
+                    stop=(b == HB - 1),
+                )
+
+        out_view = out.rearrange("(c p) s -> p c s", p=P)
+
+        def finish(q):
+            last = q == NQ - 1
+            for c in range(NC):
+                y = keep.tile([P, CH], F32, name="y%d_%d" % (q, c))
+                if last and c == 1:
+                    nc.scalar.activation(out=y[:], in_=acc[q, c][:, 0:CH], func=ACT.Identity, bias=consts[:, c, 4:5])
+                else:
+                    nc.vector.tensor_scalar(y[:], acc[q, c][:, 0:CH], consts[:, c, 4:5], None, ALU.add)
+                nc.sync.dma_start(out_view[:, c, q * CH:(q + 1) * CH], y[:])
+
+        extra = {
+            0: [lambda: order_w1_words(1), lambda: order_w1_words(2)],
+            1: [lambda: round_w2(0), lambda: gather_words(1)],
+            2: [lambda: quantize_w2(0), lambda: part_words(1), lambda: round_w2(1)],
+            3: [lambda: round_w2(2), lambda: quantize_w2(1)],
+            4: [lambda: quantize_w2(2)],
+        }
+        lag = 5
+        nu = len(units)
+        for s in range(nu + 2):
+            if s < nu:
+                densities(s, 0)
+                depths(s, 0)
+            if 1 <= s <= nu:
+                transmittances(s - 1)
+            if s < nu:
+                densities(s, 1)
+                depths(s, 1)
+            for step in extra.get(s, []):
+                step()
+            if 1 <= s <= nu:
+                gained(s - 1)
+            if s >= 2:
+                quantize_h(s - 2)
+            if s == lag:
+                for u in range(lag - 2):
+                    decode(u)
+                finish(0)
+            if s >= lag:
+                decode(s - 2)
+                if units[s - 2][1] == HB - 1:
+                    finish(units[s - 2][0])

@@ -36,51 +36,46 @@ def tile_list_voxel_transmittance_decode_kernel(tc, tab, w1_words, w1_scales, ga
         offsets = keep.tile([P, S // 16], U16, name="offsets")
         nc.sync.dma_start(offsets[:], offs)
 
-        tab_scales = keep.tile([P, T // 4], I32, name="tab_scales", align_bytes=64)
+        tab_scales = keep.tile([P, T // 4], I32, name="tab_scales", tag="first", align_bytes=64)
         nc.vector.memset(tab_scales[:], 0)
-        w1s_raw = keep.tile([P, 2, H // 4], I32, name="w1s_raw", align_bytes=64)
-        nc.vector.memset(w1s_raw[:], 0)
+        blank = keep.tile([P, 8], F32, name="blank", tag="third", align_bytes=64)
+        nc.vector.memset(blank[:], 0.0)
         rows = keep.tile([P, N], F32, name="rows")
-        nc.vector.memset(rows[:], 0.0)
+        nc.vector.tensor_copy(
+            rows[:].rearrange("p (m i) -> p m i", i=8), blank[:].unsqueeze(1).to_broadcast([P, N // 8, 8])
+        )
         vs1 = [keep.tile([P, HALF // 4], I32, name="vs1_%d" % hf, align_bytes=64) for hf in range(2)]
         for hf in range(2):
             nc.vector.memset(vs1[hf][:], 0)
+        ident = keep.tile([P, P], F32, name="ident")
+        make_identity(nc, ident[:])
+        w1s_raw = keep.tile([P, 2, H // 4], I32, name="w1s_raw", tag="second", align_bytes=64)
+        nc.gpsimd.memset(w1s_raw[:], 0)
 
-        zeros = keep.tile([P, 8], F32, name="zeros")
-        nc.gpsimd.memset(zeros[:], 0.0)
         warm = keep.tile([P, 8], F32, name="warm")
-        nc.scalar.activation(out=warm[:], in_=zeros[:], func=ACT.Exp)
+        nc.scalar.activation(out=warm[:], in_=rows[:, 0:8], func=ACT.Exp)
 
         w1_view = w1_words.rearrange("a p n -> p a n")
-        w1w_raw = [keep.tile([P, 2, 256], I32, name="w1w_raw%d" % b, align_bytes=64) for b in range(HB)]
-        nc.sync.dma_start(w1w_raw[0][:], w1_view[:, :, 0:1024].bitcast(I32))
+        w1w_first = keep.tile([P, 2, 256], I32, name="w1w_first", align_bytes=64)
+        nc.sync.dma_start(w1w_first[:], w1_view[:, :, 0:1024].bitcast(I32))
 
         scale_rows = tab[0, 512 * T:].rearrange("(h q r t) -> r q h t", h=2, q=4, r=4)
         for r in range(4):
             nc.sync.dma_start(tab_scales[r:P:16, :], scale_rows[r].bitcast(I32))
-        tab_words = keep.tile([P, T], I32, name="tab_words", align_bytes=64)
+        tab_words = keep.tile([P, T], I32, name="tab_words", tag="third", align_bytes=64)
         nc.sync.dma_start(tab_words[:], tab[0, 0:512 * T].rearrange("(p x) -> p x", p=P).bitcast(I32))
 
         for q in range(4):
-            nc.gpsimd.dma_start(
+            nc.scalar.dma_start(
                 w1s_raw[32 * q:32 * q + 4, :, :],
                 w1_scales[:, 4 * q:4 * q + 4, :].rearrange("a r c -> r a c").bitcast(I32),
             )
-        ident = keep.tile([P, P], F32, name="ident")
-        make_identity(nc, ident[:])
 
         nc.sync.dma_start(
             rows[0:4, :].rearrange("j (m i) -> j m i", i=8),
             gain.rearrange("(m j i) -> j m i", j=4, i=8),
         )
-        nc.sync.dma_start(rows[4:5, :], bias.rearrange("(o n) -> o n", o=1))
-        for b in range(1, HB):
-            nc.sync.dma_start(w1w_raw[b][:], w1_view[:, :, 1024 * b:1024 * (b + 1)].bitcast(I32))
-        w2_raw = [keep.tile([P, 4, N], F32, name="w2_raw%d" % b) for b in range(HB)]
-        w2_view = w2.rearrange("(b g j i) n -> b j g i n", b=HB, j=4, i=8)
-        for b in range(HB):
-            for j in range(4):
-                nc.sync.dma_start(w2_raw[b][:, j, :], w2_view[b, j])
+        nc.gpsimd.dma_start(rows[4:5, :], bias.rearrange("(o n) -> o n", o=1))
 
         vs0 = [keep.tile([P, HALF], U8, name="vs0_%d" % hf, align_bytes=64) for hf in range(2)]
         picked = [keep.tile([P, HALF], U32, name="picked%d" % hf, align_bytes=64) for hf in range(2)]
@@ -89,7 +84,9 @@ def tile_list_voxel_transmittance_decode_kernel(tc, tab, w1_words, w1_scales, ga
         def gather_scales(hf):
             part = offsets[:, hf * HALF // 16:(hf + 1) * HALF // 16]
             nc.vector.tensor_copy(vs0[hf][:], tab_scales[:].bitcast(U8).indirect(part))
-            nc.gpsimd.dma_start(vs1[hf][0:112, :], vs0[hf][16:P, :].bitcast(I32))
+
+        def move_scales(hf, queue):
+            queue.dma_start(vs1[hf][0:112, :], vs0[hf][16:P, :].bitcast(I32))
 
         def gather_words(hf):
             part = offsets[:, hf * HALF // 16:(hf + 1) * HALF // 16]
@@ -104,25 +101,26 @@ def tile_list_voxel_transmittance_decode_kernel(tc, tab, w1_words, w1_scales, ga
         w1w = [keep.tile([P, 2, 256], I32, name="w1w%d" % b, align_bytes=64) for b in range(HB)]
         w1s = keep.tile([P, 2 * HB, 128], I32, name="w1s", align_bytes=64)
 
+        w1w_raw = {0: w1w_first[:]}
+
         def order_w1_words(b):
-            for a in range(2):
-                nc.vector.tensor_copy(
-                    w1w[b][:, a, :].rearrange("p (j g i) -> p j g i", j=4, g=16),
-                    w1w_raw[b][:, a, :].rearrange("p (g j i) -> p j g i", j=4, g=16),
-                )
+            nc.vector.tensor_copy(
+                w1w[b][:].rearrange("p a (j g i) -> p a j g i", j=4, g=16),
+                w1w_raw[b].rearrange("p a (g j i) -> p a j g i", j=4, g=16),
+            )
 
         def order_w1_scales():
-            src = w1s_raw[:].rearrange("p a (b g j i) -> p j (a b) g i", b=HB, g=16, j=4)
-            dst = w1s[:].rearrange("p m (j g i) -> p j m g i", j=4, g=16)
-            for j in range(4):
-                nc.vector.tensor_copy(dst[:, j], src[:, j])
+            nc.vector.tensor_copy(
+                w1s[:].rearrange("p m (j g i) -> p m j g i", j=4, g=16),
+                w1s_raw[:].rearrange("p a (b g j i) -> p (a b) j g i", b=HB, g=16, j=4),
+            )
 
         w2w = keep.tile([P, HB, N], U32, name="w2w", align_bytes=64)
         w2s = keep.tile([P, HB, N], U8, name="w2s", align_bytes=64)
         w2_bf = [keep.tile([P, N, 4], BF16, name="w2_bf%d" % b, align_bytes=64) for b in range(HB)]
 
         def round_w2(b):
-            nc.vector.tensor_copy(w2_bf[b][:], w2_raw[b][:].rearrange("p j n -> p n j"))
+            nc.vector.tensor_copy(w2_bf[b][:], w2_raw[:, b].rearrange("p j n -> p n j"))
 
         def quantize_w2(b):
             flat = w2_bf[b][:].rearrange("p n j -> p (n j)")
@@ -132,9 +130,22 @@ def tile_list_voxel_transmittance_decode_kernel(tc, tab, w1_words, w1_scales, ga
                 )
 
         gather_scales(0)
+        move_scales(0, nc.scalar)
         order_w1_words(0)
         gather_scales(1)
         order_w1_scales()
+
+        w1w_rest = keep.tile([P, 2, 512], I32, name="w1w_rest", tag="first", align_bytes=64)
+        nc.sync.dma_start(w1w_rest[:], w1_view[:, :, 1024:].bitcast(I32))
+        move_scales(1, nc.sync)
+        for b in range(1, HB):
+            w1w_raw[b] = w1w_rest[:, :, 256 * (b - 1):256 * b]
+        w2_raw = keep.tile([P, HB, 4, N], F32, name="w2_raw", tag="second", align_bytes=64)
+        w2_view = w2.rearrange("(b g j i) n -> b j g i n", b=HB, j=4, i=8)
+        for b in range(HB):
+            for j in range(4):
+                nc.sync.dma_start(w2_raw[:, b, j, :], w2_view[b, j])
+
         gather_words(0)
         part_words(0)
 
@@ -144,7 +155,7 @@ def tile_list_voxel_transmittance_decode_kernel(tc, tab, w1_words, w1_scales, ga
             nc.tensor.transpose(turned[:, b, :], rows[:, P * b:P * (b + 1)], ident[:])
         nc.scalar.copy(consts[:], turned[:, 0:HB, 0:8])
 
-        units = [(q, b) for q in range(NQ) for b in range(HB)]
+        units = [(0, 0), (1, 0), (0, 1), (0, 2), (1, 1), (1, 2)] + [(q, b) for q in range(2, NQ) for b in range(HB)]
         banks, depth, trans, hb, hw, hs, acc, res = {}, {}, {}, {}, {}, {}, {}, {}
 
         def pieces(u):
@@ -230,13 +241,12 @@ def tile_list_voxel_transmittance_decode_kernel(tc, tab, w1_words, w1_scales, ga
                 nc.sync.dma_start(out_view[:, c, q * CH:(q + 1) * CH], y[:])
 
         extra = {
-            0: [lambda: order_w1_words(1), lambda: order_w1_words(2)],
-            1: [lambda: round_w2(0), lambda: gather_words(1)],
-            2: [lambda: quantize_w2(0), lambda: part_words(1), lambda: round_w2(1)],
+            0: [lambda: order_w1_words(1), lambda: gather_words(1)],
+            1: [lambda: order_w1_words(2), lambda: round_w2(0), lambda: part_words(1)],
+            2: [lambda: quantize_w2(0), lambda: round_w2(1)],
             3: [lambda: round_w2(2), lambda: quantize_w2(1)],
             4: [lambda: quantize_w2(2)],
         }
-        lag = 5
         nu = len(units)
         for s in range(nu + 2):
             if s < nu:
@@ -253,11 +263,11 @@ def tile_list_voxel_transmittance_decode_kernel(tc, tab, w1_words, w1_scales, ga
                 gained(s - 1)
             if s >= 2:
                 quantize_h(s - 2)
-            if s == lag:
-                for u in range(lag - 2):
-                    decode(u)
-                finish(0)
-            if s >= lag:
-                decode(s - 2)
-                if units[s - 2][1] == HB - 1:
-                    finish(units[s - 2][0])
+                q, b = units[s - 2]
+                if q >= 2:
+                    decode(s - 2)
+                elif b == HB - 1:
+                    for bb in range(HB):
+                        decode(units.index((q, bb)))
+                if b == HB - 1:
+                    finish(q)

@@ -21,106 +21,161 @@ P = 128
 HB = H // 512
 NC = N // P
 HALF = 512
-CH = 256
-NQ = S // CH
+BANK = 512
 
 
 def tile_list_voxel_transmittance_decode_kernel(tc, tab, w1_words, w1_scales, gain, w2, bias, offs, out):
     nc = tc.nc
     with ExitStack() as ctx:
         keep = ctx.enter_context(tc.tile_pool(name="keep", bufs=1))
+        early = ctx.enter_context(tc.tile_pool(name="early", bufs=1))
+        stage = ctx.enter_context(tc.tile_pool(name="stage", bufs=1))
         ring = ctx.enter_context(tc.tile_pool(name="ring", bufs=3))
-        psum_a = ctx.enter_context(tc.psum_pool(name="psum_a", bufs=5))
-        psum_y = ctx.enter_context(tc.psum_pool(name="psum_y", bufs=3))
+        psum = ctx.enter_context(tc.psum_pool(name="psum", bufs=1))
 
         offsets = keep.tile([P, S // 16], U16, name="offsets")
         nc.sync.dma_start(offsets[:], offs)
 
-        tab_scales = keep.tile([P, T // 4], I32, name="tab_scales", tag="first", align_bytes=64)
-        nc.vector.memset(tab_scales[:], 0)
-        blank = keep.tile([P, 8], F32, name="blank", tag="third", align_bytes=64)
-        nc.vector.memset(blank[:], 0.0)
-        rows = keep.tile([P, N], F32, name="rows")
-        nc.vector.tensor_copy(
-            rows[:].rearrange("p (m i) -> p m i", i=8), blank[:].unsqueeze(1).to_broadcast([P, N // 8, 8])
-        )
-        vs1 = [keep.tile([P, HALF // 4], I32, name="vs1_%d" % hf, align_bytes=64) for hf in range(2)]
-        for hf in range(2):
-            nc.vector.memset(vs1[hf][:], 0)
-        ident = keep.tile([P, P], F32, name="ident")
-        make_identity(nc, ident[:])
-        w1s_raw = keep.tile([P, 2, H // 4], I32, name="w1s_raw", tag="second", align_bytes=64)
-        nc.gpsimd.memset(w1s_raw[:], 0)
-
-        warm = keep.tile([P, 8], F32, name="warm")
-        nc.scalar.activation(out=warm[:], in_=rows[:, 0:8], func=ACT.Exp)
-
+        gain_rows = keep.tile([HB, 512], F32, name="gain_rows")
+        nc.gpsimd.dma_start(gain_rows[:], gain.rearrange("(b r) -> b r", b=HB))
         w1_view = w1_words.rearrange("a p n -> p a n")
-        w1w_first = keep.tile([P, 2, 256], I32, name="w1w_first", align_bytes=64)
+        w1w_first = keep.tile([P, 2, 256], I32, name="w1w_first")
         nc.sync.dma_start(w1w_first[:], w1_view[:, :, 0:1024].bitcast(I32))
 
+        tab_scales = stage.tile([P, T // 4], I32, name="tab_scales", offset=4096)
+        nc.vector.memset(tab_scales[:], 0)
         scale_rows = tab[0, 512 * T:].rearrange("(h q r t) -> r q h t", h=2, q=4, r=4)
         for r in range(4):
             nc.sync.dma_start(tab_scales[r:P:16, :], scale_rows[r].bitcast(I32))
-        tab_words = keep.tile([P, T], I32, name="tab_words", tag="third", align_bytes=64)
+
+        blank = early.tile([P, 16], F32, name="blank", offset=4 * T - 32)
+        nc.vector.memset(blank[:], 0.0)
+        rows = keep.tile([P, 512], F32, name="rows")
+        nc.vector.tensor_copy(
+            rows[:].rearrange("p (m i) -> p m i", i=16), blank[:].unsqueeze(1).to_broadcast([P, 512 // 16, 16])
+        )
+        moved_s = [keep.tile([P, HALF // 4], I32, name="moved_s%d" % hf, align_bytes=64) for hf in range(2)]
+        for hf in range(2):
+            nc.vector.memset(moved_s[hf][:], 0)
+        tab_words = early.tile([P, T], I32, name="tab_words", offset=0)
         nc.sync.dma_start(tab_words[:], tab[0, 0:512 * T].rearrange("(p x) -> p x", p=P).bitcast(I32))
 
+        ones = keep.tile([P, 8], F32, name="ones")
+        nc.gpsimd.memset(ones[:], 1.0)
+        warm_ln = keep.tile([P, 8], F32, name="warm_ln")
+        nc.scalar.activation(out=warm_ln[:], in_=ones[:], func=ACT.Ln)
+        ident = keep.tile([P, P], F32, name="ident")
+        make_identity(nc, ident[:])
+        w1s_first = early.tile([P, 2, 128], I32, name="w1s_first", offset=4 * T)
+        nc.vector.memset(w1s_first[:], 0)
+        w1s_view = w1_scales.rearrange("a r c -> r a c")
         for q in range(4):
-            nc.scalar.dma_start(
-                w1s_raw[32 * q:32 * q + 4, :, :],
-                w1_scales[:, 4 * q:4 * q + 4, :].rearrange("a r c -> r a c").bitcast(I32),
-            )
+            nc.scalar.dma_start(w1s_first[32 * q:32 * q + 4], w1s_view[4 * q:4 * q + 4, :, 0:512].bitcast(I32))
 
-        nc.sync.dma_start(
-            rows[0:4, :].rearrange("j (m i) -> j m i", i=8),
-            gain.rearrange("(m j i) -> j m i", j=4, i=8),
-        )
-        nc.gpsimd.dma_start(rows[4:5, :], bias.rearrange("(o n) -> o n", o=1))
-
-        vs0 = [keep.tile([P, HALF], U8, name="vs0_%d" % hf, align_bytes=64) for hf in range(2)]
-        picked = [keep.tile([P, HALF], U32, name="picked%d" % hf, align_bytes=64) for hf in range(2)]
+        picked_s = [keep.tile([P, HALF], U8, name="picked_s%d" % hf, align_bytes=64) for hf in range(2)]
+        picked_w = [keep.tile([P, HALF], U32, name="picked_w%d" % hf, align_bytes=64) for hf in range(2)]
         vw = [keep.tile([P, 2, 2 * HALF], U8, name="vw%d" % hf, align_bytes=64) for hf in range(2)]
 
         def gather_scales(hf):
             part = offsets[:, hf * HALF // 16:(hf + 1) * HALF // 16]
-            nc.vector.tensor_copy(vs0[hf][:], tab_scales[:].bitcast(U8).indirect(part))
+            nc.vector.tensor_copy(picked_s[hf][:], tab_scales[:].bitcast(U8).indirect(part))
 
         def move_scales(hf, queue):
-            queue.dma_start(vs1[hf][0:112, :], vs0[hf][16:P, :].bitcast(I32))
+            queue.dma_start(moved_s[hf][0:112, :], picked_s[hf][16:P, :].bitcast(I32))
 
         def gather_words(hf):
             part = offsets[:, hf * HALF // 16:(hf + 1) * HALF // 16]
-            nc.vector.tensor_copy(picked[hf][:], tab_words[:].bitcast(U32).indirect(part))
+            nc.vector.tensor_copy(picked_w[hf][:], tab_words[:].bitcast(U32).indirect(part))
 
-        def part_words(hf):
+        def part_words(hf, s0, s1):
             nc.vector.tensor_copy(
-                vw[hf][:].bitcast(U16),
-                picked[hf][:].bitcast(U16).rearrange("p (s a) -> p a s", a=2),
+                vw[hf][:, :, 2 * s0:2 * s1].bitcast(U16),
+                picked_w[hf][:, s0:s1].bitcast(U16).rearrange("p (s a) -> p a s", a=2),
             )
 
         w1w = [keep.tile([P, 2, 256], I32, name="w1w%d" % b, align_bytes=64) for b in range(HB)]
-        w1s = keep.tile([P, 2 * HB, 128], I32, name="w1s", align_bytes=64)
-
+        w1s = [keep.tile([P, 2, 128], I32, name="w1s%d" % b, align_bytes=64) for b in range(HB)]
         w1w_raw = {0: w1w_first[:]}
+        w1s_raw = {0: w1s_first[:]}
 
-        def order_w1_words(b):
+        def reorder(dst, src):
             nc.vector.tensor_copy(
-                w1w[b][:].rearrange("p a (j g i) -> p a j g i", j=4, g=16),
-                w1w_raw[b].rearrange("p a (g j i) -> p a j g i", j=4, g=16),
+                dst.rearrange("p a (j g i) -> p a j g i", j=4, g=16),
+                src.rearrange("p a (g j i) -> p a j g i", j=4, g=16),
             )
 
-        def order_w1_scales():
-            nc.vector.tensor_copy(
-                w1s[:].rearrange("p m (j g i) -> p m j g i", j=4, g=16),
-                w1s_raw[:].rearrange("p a (b g j i) -> p (a b) j g i", b=HB, g=16, j=4),
-            )
+        nc.vector.tensor_copy(
+            rows[0:HB, :].rearrange("b (j g i) -> b j g i", j=4, g=16),
+            gain_rows[:].rearrange("b (g j i) -> b j g i", j=4, g=16),
+        )
+        reorder(w1w[0][:], w1w_raw[0])
+        gather_scales(0)
+        move_scales(0, nc.scalar)
+
+        turned = psum.tile([P, 4, P], F32, name="turned", tag="y", bufs=3)
+        for j in range(4):
+            nc.tensor.transpose(turned[:, j, :], rows[:, P * j:P * (j + 1)], ident[:])
+        gains = keep.tile([P, HB, 4], F32, name="gains")
+        nc.vector.tensor_copy(gains[:], turned[:, :, 0:HB].rearrange("p j b -> p b j"))
+        flat_g = gains[:].rearrange("p b j -> p (b j)")
+        size = keep.tile([P, 4 * HB], F32, name="size")
+        nc.vector.scalar_tensor_tensor(size[:], flat_g, -1.0, flat_g, ALU.mult, ALU.max)
+        twice_negative = keep.tile([P, 4 * HB], F32, name="twice_negative")
+        nc.vector.tensor_scalar(twice_negative[:], flat_g, 0.0, -2.0, ALU.is_lt, ALU.mult)
+        down = keep.tile([P, 4 * HB], F32, name="down")
+        nc.vector.tensor_scalar(down[:], size[:], 2.0**40, 2.0**-64, ALU.is_lt, ALU.max)
+        up = keep.tile([P, 4 * HB], F32, name="up")
+        nc.vector.tensor_scalar(up[:], size[:], 2.0**-40, 2.0**62, ALU.is_lt, ALU.mult)
+        signs = keep.tile([P, HB, 4], F32, name="signs")
+        nc.vector.tensor_scalar(signs[:].rearrange("p b j -> p (b j)"), twice_negative[:], 1.0, None, ALU.add)
+        ranged = keep.tile([P, 2, 4 * HB], F32, name="ranged")
+        nc.vector.scalar_tensor_tensor(ranged[:, 1, :], up[:], 1.0, down[:], ALU.max, ALU.mult)
+        nc.vector.scalar_tensor_tensor(ranged[:, 0, :], size[:], 2.0**-126, ranged[:, 1, :], ALU.max, ALU.mult)
+        logs = keep.tile([P, 2, 4 * HB], F32, name="logs")
+        nc.scalar.activation(out=logs[:], in_=ranged[:], func=ACT.Ln)
+        warm = keep.tile([P, 8], F32, name="warm")
+        nc.scalar.activation(out=warm[:], in_=logs[:, 1, 0:8], func=ACT.Exp)
+
+        gather_scales(1)
+        reorder(w1s[0][:], w1s_raw[0])
+
+        w1_rest = stage.tile([P, 2, 768], I32, name="w1_rest", offset=0)
+        nc.vector.memset(w1_rest[:, :, 512:], 0)
+        nc.sync.dma_start(w1_rest[:, :, 0:512], w1_view[:, :, 1024:].bitcast(I32))
+        for q in range(4):
+            nc.sync.dma_start(w1_rest[32 * q:32 * q + 4, :, 512:], w1s_view[4 * q:4 * q + 4, :, 512:].bitcast(I32))
+        for b in range(1, HB):
+            w1w_raw[b] = w1_rest[:, :, 256 * (b - 1):256 * b]
+            w1s_raw[b] = w1_rest[:, :, 384 + 128 * b:512 + 128 * b]
+        w2_raw = stage.tile([P, HB, 4, N], F32, name="w2_raw", offset=6176)
+        w2_view = w2.rearrange("(b g j i) n -> b j g i n", b=HB, j=4, i=8)
+        for b in range(HB):
+            for j in range(4):
+                nc.sync.dma_start(w2_raw[:, b, j, :], w2_view[b, j])
+        move_scales(1, nc.sync)
+        biases = stage.tile([P, NC], F32, name="biases", offset=6144)
+        with nc.allow_non_contiguous_dma(reason="one bias value for each partition"):
+            nc.sync.dma_start(biases[:], bias.rearrange("(c p) -> p c", p=P))
+
+        gather_words(0)
+        part_words(0, 0, HALF // 2)
+        part_words(0, HALF // 2, HALF)
+        log_gain = keep.tile([P, HB, 4], F32, name="log_gain")
+        nc.vector.tensor_tensor(log_gain[:].rearrange("p b j -> p (b j)"), logs[:, 0, :], logs[:, 1, :], ALU.subtract)
+        half_log_gain = keep.tile([P, HB, 4], F32, name="half_log_gain")
+        nc.vector.tensor_scalar(half_log_gain[:], log_gain[:], 0.5, None, ALU.mult)
 
         w2w = keep.tile([P, HB, N], U32, name="w2w", align_bytes=64)
         w2s = keep.tile([P, HB, N], U8, name="w2s", align_bytes=64)
         w2_bf = [keep.tile([P, N, 4], BF16, name="w2_bf%d" % b, align_bytes=64) for b in range(HB)]
 
         def round_w2(b):
-            nc.vector.tensor_copy(w2_bf[b][:], w2_raw[:, b].rearrange("p j n -> p n j"))
+            nc.vector.tensor_tensor(
+                w2_bf[b][:].rearrange("p (c i) j -> p c j i", i=2),
+                w2_raw[:, b].rearrange("p j (c i) -> p c j i", i=2),
+                signs[:, b, :].unsqueeze(1).unsqueeze(3).to_broadcast([P, N // 2, 4, 2]),
+                ALU.mult,
+            )
 
         def quantize_w2(b):
             flat = w2_bf[b][:].rearrange("p n j -> p (n j)")
@@ -129,145 +184,168 @@ def tile_list_voxel_transmittance_decode_kernel(tc, tab, w1_words, w1_scales, ga
                     out=w2w[:, b, c0:c1].bitcast(FP8X4), scales=w2s[:, b, c0:c1], in_=flat[:, 4 * c0:4 * c1]
                 )
 
-        gather_scales(0)
-        move_scales(0, nc.scalar)
-        order_w1_words(0)
-        gather_scales(1)
-        order_w1_scales()
+        units = [
+            (0, 512, 0, False), (0, 512, 1, False), (0, 512, 2, False), (512, 512, 0, False),
+            (512, 256, 1, False), (512, 256, 2, False), (768, 256, 1, True), (768, 256, 2, True),
+        ]
+        banks, depth, rowwise, hb, hw, hs, acc, halves = {}, {}, {}, {}, {}, {}, {}, {}
 
-        w1w_rest = keep.tile([P, 2, 512], I32, name="w1w_rest", tag="first", align_bytes=64)
-        nc.sync.dma_start(w1w_rest[:], w1_view[:, :, 1024:].bitcast(I32))
-        move_scales(1, nc.sync)
-        for b in range(1, HB):
-            w1w_raw[b] = w1w_rest[:, :, 256 * (b - 1):256 * b]
-        w2_raw = keep.tile([P, HB, 4, N], F32, name="w2_raw", tag="second", align_bytes=64)
-        w2_view = w2.rearrange("(b g j i) n -> b j g i n", b=HB, j=4, i=8)
-        for b in range(HB):
-            for j in range(4):
-                nc.sync.dma_start(w2_raw[:, b, j, :], w2_view[b, j])
+        def densities(u, x):
+            s0, n, b = units[u][0:3]
+            per = BANK // n
+            banks[u, x] = psum.tile([P, per, n], F32, name="bank", tag="a", bufs=5)
+            for e in range(per):
+                density(banks[u, x][:, e, :], b, per * x + e, s0, n)
 
-        gather_words(0)
-        part_words(0)
-
-        consts = keep.tile([P, HB, 8], F32, name="consts")
-        turned = psum_y.tile([P, 4, P], F32, name="turned", tag="y")
-        for b in range(HB):
-            nc.tensor.transpose(turned[:, b, :], rows[:, P * b:P * (b + 1)], ident[:])
-        nc.scalar.copy(consts[:], turned[:, 0:HB, 0:8])
-
-        units = [(0, 0), (1, 0), (0, 1), (0, 2), (1, 1), (1, 2)] + [(q, b) for q in range(2, NQ) for b in range(HB)]
-        banks, depth, trans, hb, hw, hs, acc, res = {}, {}, {}, {}, {}, {}, {}, {}
-
-        def pieces(u):
-            return ((0, CH // 2), (CH // 2, CH)) if u == len(units) - 1 else ((0, CH),)
-
-        def densities(u, half):
-            q, b = units[u]
-            hf, c0 = q // 2, (q % 2) * CH
-            bank = psum_a.tile([P, 2, CH], F32, name="bank", tag="a")
-            banks[u, half] = bank
-            for e in range(2):
-                j = 2 * half + e
-                for a in range(2):
-                    plane = vs0[hf][:] if a == 0 else vs1[hf][:].bitcast(U8)
-                    nc.tensor.matmul_mx(
-                        out=bank[:, e, :],
-                        lhsT=w1w[b][:, a, 64 * j:64 * (j + 1)].bitcast(U8).bitcast(FP4X4),
-                        lhsT_scale=w1s[:, a * HB + b, 32 * j:32 * (j + 1)].bitcast(U8),
-                        rhs=vw[hf][:, a, 2 * c0:2 * (c0 + CH)].bitcast(FP4X4),
-                        rhs_scale=plane[:, c0:c0 + CH],
-                        start=(a == 0),
-                        stop=(a == 1),
-                    )
-
-        def depths(u, half):
-            if half == 0:
-                depth[u] = ring.tile([P, 2, CH, 2], F32, name="depth", tag="depth")
-            nc.scalar.activation(
-                out=depth[u][:, half], in_=banks[u, half][:].rearrange("p e n -> p n e"), func=ACT.Abs
-            )
-
-        def transmittances(u):
-            trans[u] = ring.tile([P, 2, CH, 2], F32, name="trans", tag="trans", bufs=6)
-            for n0, n1 in pieces(u):
-                nc.scalar.activation(
-                    out=trans[u][:, :, n0:n1, :], in_=depth[u][:, :, n0:n1, :], func=ACT.Exp, scale=-1.0
+        def density(into, b, j, s0, n):
+            hf, c0 = s0 // HALF, s0 % HALF
+            for a in range(2):
+                nc.tensor.matmul_mx(
+                    out=into,
+                    lhsT=w1w[b][:, a, 64 * j:64 * (j + 1)].bitcast(U8).bitcast(FP4X4),
+                    lhsT_scale=w1s[b][:, a, 32 * j:32 * (j + 1)].bitcast(U8),
+                    rhs=vw[hf][:, a, 2 * c0:2 * (c0 + n)].bitcast(FP4X4),
+                    rhs_scale=(picked_s[hf][:], moved_s[hf][:].bitcast(U8))[a][:, c0:c0 + n],
+                    start=(a == 0),
+                    stop=(a == 1),
                 )
 
-        def gained(u):
-            b = units[u][1]
-            hb[u] = ring.tile([P, CH, 2, 2], BF16, name="hb", tag="hb", align_bytes=64)
+        def depths(u, x):
+            n = units[u][1]
+            depth[u, x] = ring.tile([P, BANK // n, n], F32, name="depth", tag="depth", bufs=4)
+            nc.scalar.activation(out=depth[u, x][:], in_=banks[u, x][:], func=ACT.Abs)
+
+        def transmittances(u, x):
+            n, b = units[u][1:3]
+            per = BANK // n
+            if x == 0:
+                rowwise[u] = keep.tile([P, 4, n], BF16, name="rowwise%d" % u, align_bytes=64)
+            for e in range(per):
+                j = per * x + e
+                nc.scalar.activation(
+                    out=rowwise[u][:, j, :], in_=depth[u, x][:, e, :], func=ACT.Exp,
+                    bias=log_gain[:, b, j:j + 1], scale=-1.0,
+                )
+
+        def interleave(u):
+            n = units[u][1]
+            hb[u] = keep.tile([P, n, 4], BF16, name="hb%d" % u, align_bytes=64)
+            nc.vector.tensor_copy(
+                hb[u][:].rearrange("p (c i) j -> p c j i", i=4),
+                rowwise[u][:].rearrange("p j (c i) -> p c j i", i=4),
+            )
+
+        def exponents(u):
+            n, b = units[u][1:3]
+            depth[u] = keep.tile([P, 2, n, 2], F32, name="exponent%d" % u)
+            for x in range(2):
+                halves[u, x] = ring.tile([P, n, 2], F32, name="halves", tag="halves", bufs=2)
+                nc.vector.scalar_tensor_tensor(
+                    halves[u, x][:], banks[u, x][:].rearrange("p e n -> p n e"), 0.0,
+                    half_log_gain[:, b, 2 * x:2 * x + 2].unsqueeze(1).to_broadcast([P, n, 2]), ALU.min, ALU.add,
+                )
+            for x in range(2):
+                nc.vector.scalar_tensor_tensor(
+                    depth[u][:, x], halves[u, x][:], 2.0, banks[u, x][:].rearrange("p e n -> p n e"),
+                    ALU.mult, ALU.subtract,
+                )
+
+        def pieces(u):
+            n = units[u][1]
+            return ((0, n // 2), (n // 2, n)) if u == len(units) - 1 else ((0, n),)
+
+        def transmittances_grouped(u):
+            n = units[u][1]
+            hb[u] = keep.tile([P, n, 4], BF16, name="hb%d" % u, align_bytes=64)
             for n0, n1 in pieces(u):
-                g = consts[:, b, 0:4].rearrange("p (u e) -> p u e", u=2).unsqueeze(1).to_broadcast([P, n1 - n0, 2, 2])
-                nc.vector.tensor_tensor(
-                    hb[u][:, n0:n1], trans[u][:, :, n0:n1, :].rearrange("p u n e -> p n u e"), g, ALU.mult
+                nc.scalar.activation(
+                    out=hb[u][:, n0:n1, :].rearrange("p n (x e) -> p n x e", x=2),
+                    in_=depth[u][:, :, n0:n1, :].rearrange("p x n e -> p n x e"),
+                    func=ACT.Exp,
                 )
 
         def quantize_h(u):
-            hw[u] = keep.tile([P, CH], U32, name="hw%d" % u, align_bytes=64)
-            hs[u] = keep.tile([P, CH], U8, name="hs%d" % u, align_bytes=64)
+            n = units[u][1]
+            hw[u] = keep.tile([P, n], U32, name="hw%d" % u, align_bytes=64)
+            hs[u] = keep.tile([P, n], U8, name="hs%d" % u, align_bytes=64)
             for n0, n1 in pieces(u):
                 nc.vector.quantize_mx(
                     out=hw[u][:, n0:n1].bitcast(FP8X4),
                     scales=hs[u][:, n0:n1],
-                    in_=hb[u][:, n0:n1].rearrange("p n u e -> p (n u e)"),
+                    in_=hb[u][:, n0:n1, :].rearrange("p n j -> p (n j)"),
                 )
 
-        def decode(u):
-            q, b = units[u]
+        def decode(u, s0, n, tag, bufs):
+            b = units[u][2]
+            c0 = s0 - units[u][0]
             for c in range(NC):
                 if b == 0:
-                    acc[q, c] = psum_y.tile([P, 2 * CH], F32, name="acc", tag="y")
+                    acc[s0, c] = psum.tile([P, BANK], F32, name="acc", tag=tag, bufs=bufs)
                 nc.tensor.matmul_mx(
-                    out=acc[q, c][:, 0:CH],
+                    out=acc[s0, c][:, 0:n],
                     lhsT=w2w[:, b, P * c:P * (c + 1)].bitcast(FP8X4),
                     lhsT_scale=w2s[:, b, P * c:P * (c + 1)],
-                    rhs=hw[u][:].bitcast(FP8X4),
-                    rhs_scale=hs[u][:],
+                    rhs=hw[u][:, c0:c0 + n].bitcast(FP8X4),
+                    rhs_scale=hs[u][:, c0:c0 + n],
                     start=(b == 0),
                     stop=(b == HB - 1),
                 )
 
         out_view = out.rearrange("(c p) s -> p c s", p=P)
 
-        def finish(q):
-            last = q == NQ - 1
+        def finish(s0, n, on_scalar):
             for c in range(NC):
-                y = keep.tile([P, CH], F32, name="y%d_%d" % (q, c))
-                if last and c == 1:
-                    nc.scalar.activation(out=y[:], in_=acc[q, c][:, 0:CH], func=ACT.Identity, bias=consts[:, c, 4:5])
+                y = keep.tile([P, n], F32, name="y%d_%d" % (s0, c))
+                if c in on_scalar:
+                    nc.scalar.activation(out=y[:], in_=acc[s0, c][:, 0:n], func=ACT.Identity, bias=biases[:, c:c + 1])
                 else:
-                    nc.vector.tensor_scalar(y[:], acc[q, c][:, 0:CH], consts[:, c, 4:5], None, ALU.add)
-                nc.sync.dma_start(out_view[:, c, q * CH:(q + 1) * CH], y[:])
+                    nc.vector.tensor_scalar(y[:], acc[s0, c][:, 0:n], biases[:, c:c + 1], None, ALU.add)
+                nc.sync.dma_start(out_view[:, c, s0:s0 + n], y[:])
 
-        extra = {
-            0: [lambda: order_w1_words(1), lambda: gather_words(1)],
-            1: [lambda: order_w1_words(2), lambda: round_w2(0), lambda: part_words(1)],
-            2: [lambda: quantize_w2(0), lambda: round_w2(1)],
-            3: [lambda: round_w2(2), lambda: quantize_w2(1)],
-            4: [lambda: quantize_w2(2)],
+        slots = [(u, x) for u in range(6) for x in range(4 * units[u][1] // BANK)]
+        after = {
+            0: [lambda: gather_words(1), lambda: reorder(w1s[1][:], w1s_raw[1]), lambda: reorder(w1w[1][:], w1w_raw[1])],
+            1: [lambda: part_words(1, 0, HALF), lambda: reorder(w1s[2][:], w1s_raw[2]), lambda: reorder(w1w[2][:], w1w_raw[2])],
+            3: [lambda: round_w2(0)],
+            4: [lambda: interleave(0), lambda: quantize_w2(0), lambda: round_w2(1), lambda: quantize_h(0)],
+            6: [lambda: quantize_w2(1), lambda: round_w2(2)],
+            8: [lambda: interleave(1), lambda: quantize_w2(2), lambda: quantize_h(1)],
+            12: [lambda: interleave(2)],
+            13: [lambda: quantize_h(2), lambda: decode(0, 0, 512, "y", 3)],
+            14: [lambda: decode(1, 0, 512, "y", 3)],
+            15: [lambda: densities(6, 0), lambda: densities(6, 1), lambda: decode(2, 0, 512, "y", 3)],
+            16: [lambda: interleave(3), lambda: finish(0, 512, ()), lambda: quantize_h(3), lambda: exponents(6)],
+            18: [lambda: interleave(4)],
+            19: [
+                lambda: densities(7, 0), lambda: densities(7, 1), lambda: decode(3, 512, 256, "y", 3),
+                lambda: exponents(7), lambda: quantize_h(4),
+            ],
         }
-        nu = len(units)
-        for s in range(nu + 2):
-            if s < nu:
-                densities(s, 0)
-                depths(s, 0)
-            if 1 <= s <= nu:
-                transmittances(s - 1)
-            if s < nu:
-                densities(s, 1)
-                depths(s, 1)
-            for step in extra.get(s, []):
+        depth[0, 0] = ring.tile([P, 1, BANK], F32, name="depth", tag="depth", bufs=4)
+        for s0 in (0, BANK // 2):
+            bank = psum.tile([P, BANK // 2], F32, name="bank", tag="a", bufs=5)
+            density(bank[:], 0, 0, s0, BANK // 2)
+            nc.scalar.activation(out=depth[0, 0][:, 0, s0:s0 + BANK // 2], in_=bank[:], func=ACT.Abs)
+        transmittances(0, 0)
+        for i, (u, x) in enumerate(slots):
+            if i > 0:
+                densities(u, x)
+                depths(u, x)
+            if i > 1:
+                transmittances(*slots[i - 1])
+            for step in after.get(i, []):
                 step()
-            if 1 <= s <= nu:
-                gained(s - 1)
-            if s >= 2:
-                quantize_h(s - 2)
-                q, b = units[s - 2]
-                if q >= 2:
-                    decode(s - 2)
-                elif b == HB - 1:
-                    for bb in range(HB):
-                        decode(units.index((q, bb)))
-                if b == HB - 1:
-                    finish(q)
+        transmittances(*slots[-1])
+        transmittances_grouped(6)
+        decode(4, 512, 256, "y", 3)
+        interleave(5)
+        transmittances_grouped(7)
+        quantize_h(5)
+        quantize_h(6)
+        decode(3, 768, 256, "a", 5)
+        decode(5, 512, 256, "y", 3)
+        decode(6, 768, 256, "a", 5)
+        quantize_h(7)
+        decode(7, 768, 256, "a", 5)
+        finish(512, 256, (2,))
+        finish(768, 256, (1,))

from contextlib import ExitStack

import concourse.mybir as mybir
from concourse.masks import make_identity

K, H, N, T, S = 1024, 1536, 384, 4096, 1024
FLOPS = 2 * K * H * S + 2 * H * N * S

F32 = mybir.dt.float32
BF16 = mybir.dt.bfloat16
I32 = mybir.dt.int32
U32 = mybir.dt.uint32
U16 = mybir.dt.uint16
U8 = mybir.dt.uint8
FP8X4 = mybir.dt.float8_e4m3fn_x4
FP4X4 = mybir.dt.float4_e2m1fn_x4
ACT = mybir.ActivationFunctionType
ALU = mybir.AluOpType

P = 128
HB = H // 512
NC = N // P
HALF = 512
BANK = 512


def tile_list_voxel_transmittance_decode_kernel(tc, tab, w1_words, w1_scales, gain, w2, bias, offs, out):
    nc = tc.nc
    with ExitStack() as ctx:
        keep = ctx.enter_context(tc.tile_pool(name="keep", bufs=1))
        early = ctx.enter_context(tc.tile_pool(name="early", bufs=1))
        stage = ctx.enter_context(tc.tile_pool(name="stage", bufs=1))
        ring = ctx.enter_context(tc.tile_pool(name="ring", bufs=3))
        psum = ctx.enter_context(tc.psum_pool(name="psum", bufs=1))

        offsets = keep.tile([P, S // 16], U16, name="offsets")
        nc.sync.dma_start(offsets[:], offs)

        gain_rows = keep.tile([HB, 512], F32, name="gain_rows")
        nc.gpsimd.dma_start(gain_rows[:], gain.rearrange("(b r) -> b r", b=HB))
        w1_view = w1_words.rearrange("a p n -> p a n")
        w1w_first = keep.tile([P, 2, 256], I32, name="w1w_first")
        nc.sync.dma_start(w1w_first[:], w1_view[:, :, 0:1024].bitcast(I32))

        tab_scales = stage.tile([P, T // 4], I32, name="tab_scales", offset=4096)
        nc.vector.memset(tab_scales[:], 0)
        scale_rows = tab[0, 512 * T:].rearrange("(h q r t) -> r q h t", h=2, q=4, r=4)
        for r in range(4):
            nc.sync.dma_start(tab_scales[r:P:16, :], scale_rows[r].bitcast(I32))

        blank = early.tile([P, 16], F32, name="blank", offset=4 * T - 32)
        nc.vector.memset(blank[:], 0.0)
        rows = keep.tile([P, 512], F32, name="rows")
        nc.vector.tensor_copy(
            rows[:].rearrange("p (m i) -> p m i", i=16), blank[:].unsqueeze(1).to_broadcast([P, 512 // 16, 16])
        )
        moved_s = [keep.tile([P, HALF // 4], I32, name="moved_s%d" % hf, align_bytes=64) for hf in range(2)]
        for hf in range(2):
            nc.vector.memset(moved_s[hf][:], 0)
        tab_words = early.tile([P, T], I32, name="tab_words", offset=0)
        nc.sync.dma_start(tab_words[:], tab[0, 0:512 * T].rearrange("(p x) -> p x", p=P).bitcast(I32))

        ones = keep.tile([P, 8], F32, name="ones")
        nc.gpsimd.memset(ones[:], 1.0)
        warm_ln = keep.tile([P, 8], F32, name="warm_ln")
        nc.scalar.activation(out=warm_ln[:], in_=ones[:], func=ACT.Ln)
        ident = keep.tile([P, P], F32, name="ident")
        make_identity(nc, ident[:])
        w1s_first = early.tile([P, 2, 128], I32, name="w1s_first", offset=4 * T)
        nc.vector.memset(w1s_first[:], 0)
        w1s_view = w1_scales.rearrange("a r c -> r a c")
        for q in range(4):
            nc.scalar.dma_start(w1s_first[32 * q:32 * q + 4], w1s_view[4 * q:4 * q + 4, :, 0:512].bitcast(I32))

        picked_s = [keep.tile([P, HALF], U8, name="picked_s%d" % hf, align_bytes=64) for hf in range(2)]
        picked_w = [keep.tile([P, HALF], U32, name="picked_w%d" % hf, align_bytes=64) for hf in range(2)]
        vw = [keep.tile([P, 2, 2 * HALF], U8, name="vw%d" % hf, align_bytes=64) for hf in range(2)]

        def gather_scales(hf):
            part = offsets[:, hf * HALF // 16:(hf + 1) * HALF // 16]
            nc.vector.tensor_copy(picked_s[hf][:], tab_scales[:].bitcast(U8).indirect(part))

        def move_scales(hf, queue):
            queue.dma_start(moved_s[hf][0:112, :], picked_s[hf][16:P, :].bitcast(I32))

        def gather_words(hf):
            part = offsets[:, hf * HALF // 16:(hf + 1) * HALF // 16]
            nc.vector.tensor_copy(picked_w[hf][:], tab_words[:].bitcast(U32).indirect(part))

        def part_words(hf, s0, s1):
            nc.vector.tensor_copy(
                vw[hf][:, :, 2 * s0:2 * s1].bitcast(U16),
                picked_w[hf][:, s0:s1].bitcast(U16).rearrange("p (s a) -> p a s", a=2),
            )

        w1w = [keep.tile([P, 2, 256], I32, name="w1w%d" % b, align_bytes=64) for b in range(HB)]
        w1s = [keep.tile([P, 2, 128], I32, name="w1s%d" % b, align_bytes=64) for b in range(HB)]
        w1w_raw = {0: w1w_first[:]}
        w1s_raw = {0: w1s_first[:]}

        def reorder(dst, src):
            nc.vector.tensor_copy(
                dst.rearrange("p a (j g i) -> p a j g i", j=4, g=16),
                src.rearrange("p a (g j i) -> p a j g i", j=4, g=16),
            )

        nc.vector.tensor_copy(
            rows[0:HB, :].rearrange("b (j g i) -> b j g i", j=4, g=16),
            gain_rows[:].rearrange("b (g j i) -> b j g i", j=4, g=16),
        )
        reorder(w1w[0][:], w1w_raw[0])
        gather_scales(0)
        move_scales(0, nc.scalar)

        turned = psum.tile([P, 4, P], F32, name="turned", tag="y", bufs=3)
        for j in range(4):
            nc.tensor.transpose(turned[:, j, :], rows[:, P * j:P * (j + 1)], ident[:])
        gains = keep.tile([P, HB, 4], F32, name="gains")
        nc.vector.tensor_copy(gains[:], turned[:, :, 0:HB].rearrange("p j b -> p b j"))
        flat_g = gains[:].rearrange("p b j -> p (b j)")
        size = keep.tile([P, 4 * HB], F32, name="size")
        nc.vector.scalar_tensor_tensor(size[:], flat_g, -1.0, flat_g, ALU.mult, ALU.max)
        twice_negative = keep.tile([P, 4 * HB], F32, name="twice_negative")
        nc.vector.tensor_scalar(twice_negative[:], flat_g, 0.0, -2.0, ALU.is_lt, ALU.mult)
        down = keep.tile([P, 4 * HB], F32, name="down")
        nc.vector.tensor_scalar(down[:], size[:], 2.0**40, 2.0**-64, ALU.is_lt, ALU.max)
        up = keep.tile([P, 4 * HB], F32, name="up")
        nc.vector.tensor_scalar(up[:], size[:], 2.0**-40, 2.0**62, ALU.is_lt, ALU.mult)
        signs = keep.tile([P, HB, 4], F32, name="signs")
        nc.vector.tensor_scalar(signs[:].rearrange("p b j -> p (b j)"), twice_negative[:], 1.0, None, ALU.add)
        ranged = keep.tile([P, 2, 4 * HB], F32, name="ranged")
        nc.vector.scalar_tensor_tensor(ranged[:, 1, :], up[:], 1.0, down[:], ALU.max, ALU.mult)
        nc.vector.scalar_tensor_tensor(ranged[:, 0, :], size[:], 2.0**-126, ranged[:, 1, :], ALU.max, ALU.mult)
        logs = keep.tile([P, 2, 4 * HB], F32, name="logs")
        nc.scalar.activation(out=logs[:], in_=ranged[:], func=ACT.Ln)
        warm = keep.tile([P, 8], F32, name="warm")
        nc.scalar.activation(out=warm[:], in_=logs[:, 1, 0:8], func=ACT.Exp)

        gather_scales(1)
        reorder(w1s[0][:], w1s_raw[0])

        w1_rest = stage.tile([P, 2, 768], I32, name="w1_rest", offset=0)
        nc.vector.memset(w1_rest[:, :, 512:], 0)
        nc.sync.dma_start(w1_rest[:, :, 0:512], w1_view[:, :, 1024:].bitcast(I32))
        for q in range(4):
            nc.sync.dma_start(w1_rest[32 * q:32 * q + 4, :, 512:], w1s_view[4 * q:4 * q + 4, :, 512:].bitcast(I32))
        for b in range(1, HB):
            w1w_raw[b] = w1_rest[:, :, 256 * (b - 1):256 * b]
            w1s_raw[b] = w1_rest[:, :, 384 + 128 * b:512 + 128 * b]
        w2_raw = stage.tile([P, HB, 4, N], F32, name="w2_raw", offset=6176)
        w2_view = w2.rearrange("(b g j i) n -> b j g i n", b=HB, j=4, i=8)
        for b in range(HB):
            for j in range(4):
                nc.sync.dma_start(w2_raw[:, b, j, :], w2_view[b, j])
        move_scales(1, nc.sync)
        biases = stage.tile([P, NC], F32, name="biases", offset=6144)
        with nc.allow_non_contiguous_dma(reason="one bias value for each partition"):
            nc.sync.dma_start(biases[:], bias.rearrange("(c p) -> p c", p=P))

        gather_words(0)
        part_words(0, 0, HALF // 2)
        part_words(0, HALF // 2, HALF)
        log_gain = keep.tile([P, HB, 4], F32, name="log_gain")
        nc.vector.tensor_tensor(log_gain[:].rearrange("p b j -> p (b j)"), logs[:, 0, :], logs[:, 1, :], ALU.subtract)
        half_log_gain = keep.tile([P, HB, 4], F32, name="half_log_gain")
        nc.vector.tensor_scalar(half_log_gain[:], log_gain[:], 0.5, None, ALU.mult)

        w2w = keep.tile([P, HB, N], U32, name="w2w", align_bytes=64)
        w2s = keep.tile([P, HB, N], U8, name="w2s", align_bytes=64)
        w2_bf = [keep.tile([P, N, 4], BF16, name="w2_bf%d" % b, align_bytes=64) for b in range(HB)]

        def round_w2(b):
            nc.vector.tensor_tensor(
                w2_bf[b][:].rearrange("p (c i) j -> p c j i", i=2),
                w2_raw[:, b].rearrange("p j (c i) -> p c j i", i=2),
                signs[:, b, :].unsqueeze(1).unsqueeze(3).to_broadcast([P, N // 2, 4, 2]),
                ALU.mult,
            )

        def quantize_w2(b):
            flat = w2_bf[b][:].rearrange("p n j -> p (n j)")
            for c0, c1 in ((0, 256), (256, N)):
                nc.vector.quantize_mx(
                    out=w2w[:, b, c0:c1].bitcast(FP8X4), scales=w2s[:, b, c0:c1], in_=flat[:, 4 * c0:4 * c1]
                )

        units = [
            (0, 512, 0, False), (0, 512, 1, False), (0, 512, 2, False), (512, 512, 0, False),
            (512, 256, 1, False), (512, 256, 2, False), (768, 256, 1, True), (768, 256, 2, True),
        ]
        banks, depth, rowwise, hb, hw, hs, acc, halves = {}, {}, {}, {}, {}, {}, {}, {}

        def densities(u, x):
            s0, n, b = units[u][0:3]
            per = BANK // n
            banks[u, x] = psum.tile([P, per, n], F32, name="bank", tag="a", bufs=5)
            for e in range(per):
                density(banks[u, x][:, e, :], b, per * x + e, s0, n)

        def density(into, b, j, s0, n):
            hf, c0 = s0 // HALF, s0 % HALF
            for a in range(2):
                nc.tensor.matmul_mx(
                    out=into,
                    lhsT=w1w[b][:, a, 64 * j:64 * (j + 1)].bitcast(U8).bitcast(FP4X4),
                    lhsT_scale=w1s[b][:, a, 32 * j:32 * (j + 1)].bitcast(U8),
                    rhs=vw[hf][:, a, 2 * c0:2 * (c0 + n)].bitcast(FP4X4),
                    rhs_scale=(picked_s[hf][:], moved_s[hf][:].bitcast(U8))[a][:, c0:c0 + n],
                    start=(a == 0),
                    stop=(a == 1),
                )

        def depths(u, x):
            n = units[u][1]
            depth[u, x] = ring.tile([P, BANK // n, n], F32, name="depth", tag="depth", bufs=4)
            nc.scalar.activation(out=depth[u, x][:], in_=banks[u, x][:], func=ACT.Abs)

        def transmittances(u, x):
            n, b = units[u][1:3]
            per = BANK // n
            if x == 0:
                rowwise[u] = keep.tile([P, 4, n], BF16, name="rowwise%d" % u, align_bytes=64)
            for e in range(per):
                j = per * x + e
                nc.scalar.activation(
                    out=rowwise[u][:, j, :], in_=depth[u, x][:, e, :], func=ACT.Exp,
                    bias=log_gain[:, b, j:j + 1], scale=-1.0,
                )

        def interleave(u):
            n = units[u][1]
            hb[u] = keep.tile([P, n, 4], BF16, name="hb%d" % u, align_bytes=64)
            nc.vector.tensor_copy(
                hb[u][:].rearrange("p (c i) j -> p c j i", i=4),
                rowwise[u][:].rearrange("p j (c i) -> p c j i", i=4),
            )

        def exponents(u):
            n, b = units[u][1:3]
            depth[u] = keep.tile([P, 2, n, 2], F32, name="exponent%d" % u)
            for x in range(2):
                halves[u, x] = ring.tile([P, n, 2], F32, name="halves", tag="halves", bufs=2)
                nc.vector.scalar_tensor_tensor(
                    halves[u, x][:], banks[u, x][:].rearrange("p e n -> p n e"), 0.0,
                    half_log_gain[:, b, 2 * x:2 * x + 2].unsqueeze(1).to_broadcast([P, n, 2]), ALU.min, ALU.add,
                )
            for x in range(2):
                nc.vector.scalar_tensor_tensor(
                    depth[u][:, x], halves[u, x][:], 2.0, banks[u, x][:].rearrange("p e n -> p n e"),
                    ALU.mult, ALU.subtract,
                )

        def pieces(u):
            n = units[u][1]
            return ((0, n // 2), (n // 2, n)) if u == len(units) - 1 else ((0, n),)

        def transmittances_grouped(u):
            n = units[u][1]
            hb[u] = keep.tile([P, n, 4], BF16, name="hb%d" % u, align_bytes=64)
            for n0, n1 in pieces(u):
                nc.scalar.activation(
                    out=hb[u][:, n0:n1, :].rearrange("p n (x e) -> p n x e", x=2),
                    in_=depth[u][:, :, n0:n1, :].rearrange("p x n e -> p n x e"),
                    func=ACT.Exp,
                )

        def quantize_h(u):
            n = units[u][1]
            hw[u] = keep.tile([P, n], U32, name="hw%d" % u, align_bytes=64)
            hs[u] = keep.tile([P, n], U8, name="hs%d" % u, align_bytes=64)
            for n0, n1 in pieces(u):
                nc.vector.quantize_mx(
                    out=hw[u][:, n0:n1].bitcast(FP8X4),
                    scales=hs[u][:, n0:n1],
                    in_=hb[u][:, n0:n1, :].rearrange("p n j -> p (n j)"),
                )

        def decode(u, s0, n, tag, bufs):
            b = units[u][2]
            c0 = s0 - units[u][0]
            for c in range(NC):
                if b == 0:
                    acc[s0, c] = psum.tile([P, BANK], F32, name="acc", tag=tag, bufs=bufs)
                nc.tensor.matmul_mx(
                    out=acc[s0, c][:, 0:n],
                    lhsT=w2w[:, b, P * c:P * (c + 1)].bitcast(FP8X4),
                    lhsT_scale=w2s[:, b, P * c:P * (c + 1)],
                    rhs=hw[u][:, c0:c0 + n].bitcast(FP8X4),
                    rhs_scale=hs[u][:, c0:c0 + n],
                    start=(b == 0),
                    stop=(b == HB - 1),
                )

        out_view = out.rearrange("(c p) s -> p c s", p=P)

        def finish(s0, n, on_scalar):
            for c in range(NC):
                y = keep.tile([P, n], F32, name="y%d_%d" % (s0, c))
                if c in on_scalar:
                    nc.scalar.activation(out=y[:], in_=acc[s0, c][:, 0:n], func=ACT.Identity, bias=biases[:, c:c + 1])
                else:
                    nc.vector.tensor_scalar(y[:], acc[s0, c][:, 0:n], biases[:, c:c + 1], None, ALU.add)
                nc.sync.dma_start(out_view[:, c, s0:s0 + n], y[:])

        slots = [(u, x) for u in range(6) for x in range(4 * units[u][1] // BANK)]
        after = {
            0: [lambda: gather_words(1), lambda: reorder(w1s[1][:], w1s_raw[1]), lambda: reorder(w1w[1][:], w1w_raw[1])],
            1: [lambda: part_words(1, 0, HALF), lambda: reorder(w1s[2][:], w1s_raw[2]), lambda: reorder(w1w[2][:], w1w_raw[2])],
            3: [lambda: round_w2(0)],
            4: [lambda: interleave(0), lambda: quantize_w2(0), lambda: round_w2(1), lambda: quantize_h(0)],
            6: [lambda: quantize_w2(1), lambda: round_w2(2)],
            8: [lambda: interleave(1), lambda: quantize_w2(2), lambda: quantize_h(1)],
            12: [lambda: interleave(2)],
            13: [lambda: quantize_h(2), lambda: decode(0, 0, 512, "y", 3)],
            14: [lambda: decode(1, 0, 512, "y", 3)],
            15: [lambda: densities(6, 0), lambda: densities(6, 1), lambda: decode(2, 0, 512, "y", 3)],
            16: [lambda: interleave(3), lambda: finish(0, 512, ()), lambda: quantize_h(3), lambda: exponents(6)],
            18: [lambda: interleave(4)],
            19: [
                lambda: densities(7, 0), lambda: densities(7, 1), lambda: decode(3, 512, 256, "y", 3),
                lambda: exponents(7), lambda: quantize_h(4),
            ],
        }
        depth[0, 0] = ring.tile([P, 1, BANK], F32, name="depth", tag="depth", bufs=4)
        for s0 in (0, BANK // 2):
            bank = psum.tile([P, BANK // 2], F32, name="bank", tag="a", bufs=5)
            density(bank[:], 0, 0, s0, BANK // 2)
            nc.scalar.activation(out=depth[0, 0][:, 0, s0:s0 + BANK // 2], in_=bank[:], func=ACT.Abs)
        transmittances(0, 0)
        for i, (u, x) in enumerate(slots):
            if i > 0:
                densities(u, x)
                depths(u, x)
            if i > 1:
                transmittances(*slots[i - 1])
            for step in after.get(i, []):
                step()
        transmittances(*slots[-1])
        transmittances_grouped(6)
        decode(4, 512, 256, "y", 3)
        interleave(5)
        transmittances_grouped(7)
        quantize_h(5)
        quantize_h(6)
        decode(3, 768, 256, "a", 5)
        decode(5, 512, 256, "y", 3)
        decode(6, 768, 256, "a", 5)
        quantize_h(7)
        decode(7, 768, 256, "a", 5)
        finish(512, 256, (2,))
        finish(768, 256, (1,))
